import numpy as np
import ml_dtypes


def mxq(x, axis, fmt="e4m3"):
    dtype, down = {"e4m3": (ml_dtypes.float8_e4m3fn, 7), "e5m2": (ml_dtypes.float8_e5m2, 14)}[fmt]
    v = np.moveaxis(np.asarray(x, np.float32).astype(ml_dtypes.bfloat16).astype(np.float64), axis, -1)
    blocks = v.reshape(v.shape[:-1] + (-1, 32))
    amax = np.abs(blocks).max(-1, keepdims=True)
    byte = np.maximum(np.where(amax > 0, np.frexp(amax)[1] - 1 + 127, 0) - down, 1)
    scale = np.exp2(byte - 127.0)
    codes = (blocks / scale).astype(np.float32).astype(dtype).astype(np.float64)
    return np.moveaxis((codes * scale).reshape(v.shape), -1, axis)


WIDE = False


def mx_kscale(k):
    if not WIDE:
        return np.ones(k)
    levels = np.array([10, -10, 5, -5, 0])
    if k % 512:
        return np.exp2(np.random.permutation(np.resize(levels, k // 32))).repeat(32)
    a = np.empty((k // 512, 16))
    for p in range(k // 512):
        a[p, :8] = np.random.permutation(np.resize(levels, 8))
        for g in range(8):
            far = levels[np.abs(levels - a[p, g]) >= 10]
            a[p, g + 8] = far[np.random.randint(len(far))]
    return np.exp2(a.ravel()).repeat(32)


def f64(x):
    return np.asarray(x).astype(np.float64)


def striped8(idx):
    return np.asarray(idx).reshape(8, -1, 16).transpose(0, 2, 1).reshape(128, -1).astype(np.uint16)


def unstriped8(offs):
    return offs.reshape(8, 16, -1).transpose(0, 2, 1).reshape(8, -1).astype(np.int64)


def pick8(x, idx, run):
    r = np.arange(len(x))
    return x[r[:, None], idx[r % (8 * run) // run]]


E2M1 = np.array([0.0, 0.5, 1.0, 1.5, 2.0, 3.0, 4.0, 6.0, -0.0, -0.5, -1.0, -1.5, -2.0, -3.0, -4.0, -6.0])


def pack_weight(w, fmt):
    k, n = w.shape
    w = f64(np.asarray(w, np.float32).astype(ml_dtypes.bfloat16)).reshape(k // 32, 32, n)
    amax = np.abs(w).max(1)
    if fmt == "e4m3":
        byte = np.frexp(amax)[1] - 1 + 127 - 7
    else:
        mant, ex = np.frexp(amax / 6.0)
        byte = np.where(mant > 0.5, ex, ex - 1) + 127
    byte = np.clip(np.where(amax > 0, byte, 1), 1, 254)
    scaled = (w * np.exp2(127.0 - byte)[:, None, :]).reshape(k, n).astype(np.float32)
    by_word = np.ascontiguousarray(scaled.reshape(k // 512, 128, 4, n).transpose(0, 1, 3, 2))
    if fmt == "e4m3":
        words = by_word.astype(ml_dtypes.float8_e4m3fn).view(np.uint8)
    else:
        c = by_word.astype(ml_dtypes.float4_e2m1fn).view(np.uint8) & 0xF
        words = (c[..., 0::2] | (c[..., 1::2] << 4)).reshape(k // 512, 128, 2 * n)
    return np.ascontiguousarray(words), np.ascontiguousarray(byte.astype(np.uint8).reshape(k // 512, 16, n))


def unpack_weight(words, scales, fmt):
    g, _, n = scales.shape
    words = np.ascontiguousarray(words).reshape(g, 128, n, -1)
    if fmt == "e4m3":
        vals = words.view(ml_dtypes.float8_e4m3fn).astype(np.float64)
    else:
        nib = np.empty((g, 128, n, 4), np.uint8)
        nib[..., 0::2] = words & 0xF
        nib[..., 1::2] = words >> 4
        vals = E2M1[nib]
    vals = vals * np.repeat(np.exp2(scales.astype(np.float64) - 127.0), 8, axis=1)[..., None]
    return vals.transpose(0, 1, 3, 2).reshape(g * 512, n)


def sigmoid(v):
    return 1.0 / (1.0 + np.exp(-v))


D, T, U, X, I, Q = 512, 1024, 1024, 1024, 512, 128


def setup_inputs():
    n = np.random.standard_normal
    idx = np.stack([np.random.permutation(T)[:I] for _ in range(8)])
    idx2 = np.stack([np.random.permutation(X)[:I] for _ in range(8)])
    idx3 = np.stack([np.random.permutation(U)[:I] for _ in range(8)])
    idx4 = np.stack([np.random.permutation(U)[:I] for _ in range(8)])
    idx5 = np.stack([np.random.permutation(T)[:I] for _ in range(8)])
    fd = mx_kscale(D)
    keysp = pack_weight(n((D, T)) / fd[:, None], "e2m1")
    notesp = pack_weight(n((D, U)) / fd[:, None], "e4m3")
    usersp = pack_weight(n((D, X)) / fd[:, None], "e2m1")
    return {
        "query": (n((D, Q)) * 1.0 / np.sqrt(D) * fd[:, None]).astype(np.float32),
        "keys_words": keysp[0],
        "keys_scales": keysp[1],
        "notes_words": notesp[0],
        "notes_scales": notesp[1],
        "users_words": usersp[0],
        "users_scales": usersp[1],
        "thr": (np.random.uniform(-0.6, 0.6, (Q, 1))).astype(np.float32),
        "slope": (np.random.uniform(1.0, 3.0, (Q, 1))).astype(np.float32),
        "offs": striped8(idx),
        "offs2": striped8(idx2),
        "offs3": striped8(idx3),
        "offs4": striped8(idx4),
        "offs5": striped8(idx5),
    }


def reference(query, keys_words, keys_scales, notes_words, notes_scales, users_words, users_scales, thr, slope, offs, offs2, offs3, offs4, offs5):
    idx = unstriped8(offs)
    idx2 = unstriped8(offs2)
    idx3 = unstriped8(offs3)
    idx4 = unstriped8(offs4)
    idx5 = unstriped8(offs5)
    keysu = unpack_weight(keys_words, keys_scales, "e2m1")
    notesu = unpack_weight(notes_words, notes_scales, "e4m3")
    usersu = unpack_weight(users_words, users_scales, "e2m1")
    queryq = mxq(f64(query), 0, "e4m3")
    a = queryq.T @ keysu
    b = queryq.T @ notesu
    c0 = queryq.T @ usersu
    s1 = sigmoid(pick8(a, idx, 16) * f64(slope) + f64(thr))
    w = pick8(c0, idx2, 16) * s1
    f1 = np.zeros((Q, U))
    f1[np.arange(Q)[:, None], idx3[np.arange(Q) % 128 // 16]] = w
    cc = b + f1
    y = np.maximum(pick8(cc, idx4, 16), pick8(a, idx5, 16))
    return y

@@ -1,0 +1,154 @@
+from contextlib import ExitStack
+
+import concourse.mybir as mybir
+
+F32 = mybir.dt.float32
+BF16 = mybir.dt.bfloat16
+I32 = mybir.dt.int32
+U32 = mybir.dt.uint32
+U16 = mybir.dt.uint16
+U8 = mybir.dt.uint8
+FP8X4 = mybir.dt.float8_e4m3fn_x4
+FP4X4 = mybir.dt.float4_e2m1fn_x4
+ACT = mybir.ActivationFunctionType
+ALU = mybir.AluOpType
+
+P = 128
+PACK = 4
+POOL = 1024
+SLOTS = 512
+GROUP = 16
+PIECE = 256
+BANK = 512
+HALF = SLOTS // 2
+FIRST = 128
+SHARE = 288
+
+FLOPS = 2 * 512 * 128 * 3 * POOL
+
+
+def offsets(tile, lo, hi):
+    return tile[:, lo // GROUP : hi // GROUP]
+
+
+def tile_attend_upheld_three_kernel(tc, query, keys_words, keys_scales, notes_words, notes_scales,
+                                     users_words, users_scales, thr, slope,
+                                     offs, offs2, offs3, offs4, offs5, out):
+    nc = tc.nc
+    with ExitStack() as ctx:
+        lists = ctx.enter_context(tc.tile_pool(name="lists", bufs=1))
+        sb = ctx.enter_context(tc.tile_pool(name="sb", bufs=1))
+        ps = ctx.enter_context(tc.psum_pool(name="ps", bufs=1))
+
+        def load_list(src, name):
+            tile = lists.tile([P, SLOTS // GROUP], U16, name=name)
+            nc.sync.dma_start(tile[:], src)
+            return tile
+
+        def zeroed_plane(name):
+            plane = sb.tile([P, POOL], U8, name=name, align_bytes=64)
+            nc.vector.memset(plane[:].bitcast(I32), 0)
+            return plane
+
+        def load_scale_rows(queue, plane, src, quad):
+            queue.dma_start(plane[32 * quad : 32 * quad + 4, :].bitcast(I32),
+                            src[0, 4 * quad : 4 * quad + 4, :].bitcast(I32))
+
+        def load_words(src, width, name):
+            words = sb.tile([P, width], U8, name=name, align_bytes=64)
+            nc.sync.dma_start(words[:].bitcast(I32), src.bitcast(I32))
+            return words
+
+        def load_column(queue, src, name):
+            col = sb.tile([P, 1], F32, name=name)
+            queue.dma_start(col[:], src)
+            return col
+
+        k_plane = zeroed_plane("k_plane")
+        u_plane = zeroed_plane("u_plane")
+        n_plane = zeroed_plane("n_plane")
+        q_raw = sb.tile([P, PACK, P], F32, name="q_raw")
+        nc.sync.dma_start(q_raw[:], query.rearrange("(p j) w -> p j w", j=PACK))
+        load_scale_rows(nc.sync, k_plane, keys_scales, 0)
+        load_scale_rows(nc.sync, k_plane, keys_scales, 1)
+        load_scale_rows(nc.sync, k_plane, keys_scales, 2)
+        load_scale_rows(nc.sync, k_plane, keys_scales, 3)
+        k_words = load_words(keys_words[0], 2 * POOL, "k_words")
+        u_words = load_words(users_words[0], 2 * POOL, "u_words")
+        load_scale_rows(nc.sync, u_plane, users_scales, 0)
+        load_scale_rows(nc.sync, u_plane, users_scales, 1)
+        load_scale_rows(nc.sync, u_plane, users_scales, 2)
+        load_scale_rows(nc.sync, u_plane, users_scales, 3)
+        l1 = load_list(offs, "l1")
+        thr_t = load_column(nc.sync, thr, "thr_t")
+        slope_t = load_column(nc.sync, slope, "slope_t")
+        l2 = load_list(offs2, "l2")
+        l3 = load_list(offs3, "l3")
+        n_words = load_words(notes_words[0].rearrange("p n t -> p (n t)"), 4 * POOL, "n_words")
+        load_scale_rows(nc.sync, n_plane, notes_scales, 0)
+        load_scale_rows(nc.sync, n_plane, notes_scales, 1)
+        load_scale_rows(nc.sync, n_plane, notes_scales, 2)
+        load_scale_rows(nc.sync, n_plane, notes_scales, 3)
+        l5 = load_list(offs5, "l5")
+        l4 = load_list(offs4, "l4")
+
+        f1 = sb.tile([P, POOL], F32, name="f1")
+        nc.vector.memset(f1[:], 0.0)
+
+        q_bf = sb.tile([P, P, PACK], BF16, name="q_bf", align_bytes=64)
+        for copy, lo, hi in ((nc.vector.tensor_copy, 0, 64), (nc.scalar.copy, 64, P)):
+            copy(out=q_bf[:, lo:hi, :].rearrange("p (c i) t -> p c t i", i=4),
+                 in_=q_raw[:, :, lo:hi].rearrange("p t (c i) -> p c t i", i=4))
+        q_codes = sb.tile([P, P], U32, name="q_codes", align_bytes=64)
+        q_plane = sb.tile([P, P], U8, name="q_plane", align_bytes=64)
+        nc.vector.quantize_mx(out=q_codes[:].bitcast(FP8X4), scales=q_plane[:],
+                              in_=q_bf[:].rearrange("p w j -> p (w j)"))
+
+        def score(bank, words, plane, lo, hi, dtype, width):
+            acc = ps.tile([P, hi - lo], F32, name="acc", tag="bank%d" % bank)
+            nc.tensor.matmul_mx(out=acc[:], lhsT=q_codes[:].bitcast(FP8X4), lhsT_scale=q_plane[:],
+                                rhs=words[:, width * lo : width * hi].bitcast(dtype),
+                                rhs_scale=plane[:, lo:hi], start=True, stop=True)
+            return acc
+
+        copies = {"v": nc.vector.tensor_copy, "s": nc.scalar.copy}
+        a = sb.tile([P, POOL], F32, name="a")
+        for j in range(POOL // PIECE):
+            acc = score(j, k_words, k_plane, j * PIECE, (j + 1) * PIECE, FP4X4, 2)
+            copies["vsvs"[j]](out=a[:, j * PIECE : (j + 1) * PIECE], in_=acc[:])
+        c0 = sb.tile([P, POOL], F32, name="c0", tag="c0")
+        for j in range(POOL // PIECE):
+            acc = score(POOL // PIECE + j, u_words, u_plane, j * PIECE, (j + 1) * PIECE, FP4X4, 2)
+            copies["vvvv"[j]](out=c0[:, j * PIECE : (j + 1) * PIECE], in_=acc[:])
+        b = [score(j, n_words, n_plane, j * BANK, (j + 1) * BANK, FP8X4, 4) for j in range(POOL // BANK)]
+
+        s1 = sb.tile([P, SLOTS], F32, name="s1")
+        for lo in (0, HALF):
+            nc.scalar.activation(s1[:, lo : lo + HALF], a[:].indirect(offsets(l1, lo, lo + HALF)),
+                                 ACT.Sigmoid, bias=thr_t[:], scale=slope_t[:])
+
+        w_first = sb.tile([P, FIRST], F32, name="w_first")
+        nc.vector.tensor_tensor(w_first[:], c0[:].indirect(offsets(l2, 0, FIRST)), s1[:, :FIRST], ALU.mult)
+        c_rest = sb.tile([P, SLOTS - FIRST], F32, name="c_rest")
+        nc.scalar.activation(c_rest[:], c0[:].indirect(offsets(l2, FIRST, SLOTS)), ACT.Copy)
+        nc.vector.tensor_copy(f1[:].indirect(offsets(l3, 0, FIRST)), w_first[:])
+        nc.vector.tensor_tensor(f1[:].indirect(offsets(l3, FIRST, SLOTS)), c_rest[:], s1[:, FIRST:], ALU.mult)
+
+        late = sb.tile([P, SLOTS + SHARE], F32, name="late", tag="c0")
+        a5 = late[:, :SLOTS]
+        b_share = late[:, SLOTS:]
+        nc.scalar.activation(a5, a[:].indirect(l5[:]), ACT.Copy)
+        nc.scalar.copy(out=b_share, in_=b[1][:, BANK - SHARE :])
+
+        cc = sb.tile([P, POOL], F32, name="cc")
+        nc.gpsimd.tensor_tensor(cc[:, POOL - SHARE :], b_share, f1[:, POOL - SHARE :], ALU.add)
+        nc.vector.tensor_tensor(cc[:, :BANK], b[0][:], f1[:, :BANK], ALU.add)
+        nc.vector.tensor_tensor(cc[:, BANK : POOL - SHARE], b[1][:, : BANK - SHARE], f1[:, BANK : POOL - SHARE], ALU.add)
+
+        c4 = sb.tile([P, SLOTS], F32, name="c4")
+        nc.vector.tensor_copy(c4[:, :HALF], cc[:].indirect(offsets(l4, 0, HALF)))
+        nc.scalar.activation(c4[:, HALF:], cc[:].indirect(offsets(l4, HALF, SLOTS)), ACT.Copy)
+        y = sb.tile([P, SLOTS], F32, name="y")
+        for lo, hi, queue in ((0, HALF, nc.sync), (HALF, SLOTS, nc.scalar)):
+            nc.vector.tensor_tensor(y[:, lo:hi], c4[:, lo:hi], a5[:, lo:hi], ALU.max)
+            queue.dma_start(out[:, lo:hi], y[:, lo:hi])

@@ -67,6 +67,10 @@ def tile_attend_upheld_three_kernel(tc, query, keys_words, keys_scales, notes_wo
         k_plane = zeroed_plane("k_plane")
         u_plane = zeroed_plane("u_plane")
         n_plane = zeroed_plane("n_plane")
+        scratch = sb.tile([P, 1], F32, name="scratch")
+        nc.gpsimd.memset(scratch[:], 0.0)
+        unread = sb.tile([P, 1], F32, name="unread")
+        nc.scalar.activation(unread[:], scratch[:], ACT.Sigmoid)
         q_raw = sb.tile([P, PACK, P], F32, name="q_raw")
         nc.sync.dma_start(q_raw[:], query.rearrange("(p j) w -> p j w", j=PACK))
         load_scale_rows(nc.sync, k_plane, keys_scales, 0)

@@ -73,6 +73,7 @@ def tile_attend_upheld_three_kernel(tc, query, keys_words, keys_scales, notes_wo
         nc.scalar.activation(unread[:], scratch[:], ACT.Sigmoid)
         q_raw = sb.tile([P, PACK, P], F32, name="q_raw")
         nc.sync.dma_start(q_raw[:], query.rearrange("(p j) w -> p j w", j=PACK))
+        l1 = load_list(offs, "l1")
         load_scale_rows(nc.sync, k_plane, keys_scales, 0)
         load_scale_rows(nc.sync, k_plane, keys_scales, 1)
         load_scale_rows(nc.sync, k_plane, keys_scales, 2)
@@ -83,7 +84,6 @@ def tile_attend_upheld_three_kernel(tc, query, keys_words, keys_scales, notes_wo
         load_scale_rows(nc.sync, u_plane, users_scales, 1)
         load_scale_rows(nc.sync, u_plane, users_scales, 2)
         load_scale_rows(nc.sync, u_plane, users_scales, 3)
-        l1 = load_list(offs, "l1")
         thr_t = load_column(nc.sync, thr, "thr_t")
         slope_t = load_column(nc.sync, slope, "slope_t")
         l2 = load_list(offs2, "l2")

from contextlib import ExitStack

import concourse.mybir as mybir

F32 = mybir.dt.float32
BF16 = mybir.dt.bfloat16
I32 = mybir.dt.int32
U32 = mybir.dt.uint32
U16 = mybir.dt.uint16
U8 = mybir.dt.uint8
FP8X4 = mybir.dt.float8_e4m3fn_x4
FP4X4 = mybir.dt.float4_e2m1fn_x4
ACT = mybir.ActivationFunctionType
ALU = mybir.AluOpType

P = 128
PACK = 4
POOL = 1024
SLOTS = 512
GROUP = 16
PIECE = 256
BANK = 512
HALF = SLOTS // 2
FIRST = 128
SHARE = 288

FLOPS = 2 * 512 * 128 * 3 * POOL


def offsets(tile, lo, hi):
    return tile[:, lo // GROUP : hi // GROUP]


def tile_attend_upheld_three_kernel(tc, query, keys_words, keys_scales, notes_words, notes_scales,
                                     users_words, users_scales, thr, slope,
                                     offs, offs2, offs3, offs4, offs5, out):
    nc = tc.nc
    with ExitStack() as ctx:
        lists = ctx.enter_context(tc.tile_pool(name="lists", bufs=1))
        sb = ctx.enter_context(tc.tile_pool(name="sb", bufs=1))
        ps = ctx.enter_context(tc.psum_pool(name="ps", bufs=1))

        def load_list(src, name):
            tile = lists.tile([P, SLOTS // GROUP], U16, name=name)
            nc.sync.dma_start(tile[:], src)
            return tile

        def zeroed_plane(name):
            plane = sb.tile([P, POOL], U8, name=name, align_bytes=64)
            nc.vector.memset(plane[:].bitcast(I32), 0)
            return plane

        def load_scale_rows(queue, plane, src, quad):
            queue.dma_start(plane[32 * quad : 32 * quad + 4, :].bitcast(I32),
                            src[0, 4 * quad : 4 * quad + 4, :].bitcast(I32))

        def load_words(src, width, name):
            words = sb.tile([P, width], U8, name=name, align_bytes=64)
            nc.sync.dma_start(words[:].bitcast(I32), src.bitcast(I32))
            return words

        def load_column(queue, src, name):
            col = sb.tile([P, 1], F32, name=name)
            queue.dma_start(col[:], src)
            return col

        k_plane = zeroed_plane("k_plane")
        u_plane = zeroed_plane("u_plane")
        n_plane = zeroed_plane("n_plane")
        scratch = sb.tile([P, 1], F32, name="scratch")
        nc.gpsimd.memset(scratch[:], 0.0)
        unread = sb.tile([P, 1], F32, name="unread")
        nc.scalar.activation(unread[:], scratch[:], ACT.Sigmoid)
        q_raw = sb.tile([P, PACK, P], F32, name="q_raw")
        nc.sync.dma_start(q_raw[:], query.rearrange("(p j) w -> p j w", j=PACK))
        l1 = load_list(offs, "l1")
        load_scale_rows(nc.sync, k_plane, keys_scales, 0)
        load_scale_rows(nc.sync, k_plane, keys_scales, 1)
        load_scale_rows(nc.sync, k_plane, keys_scales, 2)
        load_scale_rows(nc.sync, k_plane, keys_scales, 3)
        k_words = load_words(keys_words[0], 2 * POOL, "k_words")
        u_words = load_words(users_words[0], 2 * POOL, "u_words")
        load_scale_rows(nc.sync, u_plane, users_scales, 0)
        load_scale_rows(nc.sync, u_plane, users_scales, 1)
        load_scale_rows(nc.sync, u_plane, users_scales, 2)
        load_scale_rows(nc.sync, u_plane, users_scales, 3)
        thr_t = load_column(nc.sync, thr, "thr_t")
        slope_t = load_column(nc.sync, slope, "slope_t")
        l2 = load_list(offs2, "l2")
        l3 = load_list(offs3, "l3")
        n_words = load_words(notes_words[0].rearrange("p n t -> p (n t)"), 4 * POOL, "n_words")
        load_scale_rows(nc.sync, n_plane, notes_scales, 0)
        load_scale_rows(nc.sync, n_plane, notes_scales, 1)
        load_scale_rows(nc.sync, n_plane, notes_scales, 2)
        load_scale_rows(nc.sync, n_plane, notes_scales, 3)
        l5 = load_list(offs5, "l5")
        l4 = load_list(offs4, "l4")

        f1 = sb.tile([P, POOL], F32, name="f1")
        nc.vector.memset(f1[:], 0.0)

        q_bf = sb.tile([P, P, PACK], BF16, name="q_bf", align_bytes=64)
        for copy, lo, hi in ((nc.vector.tensor_copy, 0, 64), (nc.scalar.copy, 64, P)):
            copy(out=q_bf[:, lo:hi, :].rearrange("p (c i) t -> p c t i", i=4),
                 in_=q_raw[:, :, lo:hi].rearrange("p t (c i) -> p c t i", i=4))
        q_codes = sb.tile([P, P], U32, name="q_codes", align_bytes=64)
        q_plane = sb.tile([P, P], U8, name="q_plane", align_bytes=64)
        nc.vector.quantize_mx(out=q_codes[:].bitcast(FP8X4), scales=q_plane[:],
                              in_=q_bf[:].rearrange("p w j -> p (w j)"))

        def score(bank, words, plane, lo, hi, dtype, width):
            acc = ps.tile([P, hi - lo], F32, name="acc", tag="bank%d" % bank)
            nc.tensor.matmul_mx(out=acc[:], lhsT=q_codes[:].bitcast(FP8X4), lhsT_scale=q_plane[:],
                                rhs=words[:, width * lo : width * hi].bitcast(dtype),
                                rhs_scale=plane[:, lo:hi], start=True, stop=True)
            return acc

        copies = {"v": nc.vector.tensor_copy, "s": nc.scalar.copy}
        a = sb.tile([P, POOL], F32, name="a")
        for j in range(POOL // PIECE):
            acc = score(j, k_words, k_plane, j * PIECE, (j + 1) * PIECE, FP4X4, 2)
            copies["vsvs"[j]](out=a[:, j * PIECE : (j + 1) * PIECE], in_=acc[:])
        c0 = sb.tile([P, POOL], F32, name="c0", tag="c0")
        for j in range(POOL // PIECE):
            acc = score(POOL // PIECE + j, u_words, u_plane, j * PIECE, (j + 1) * PIECE, FP4X4, 2)
            copies["vvvv"[j]](out=c0[:, j * PIECE : (j + 1) * PIECE], in_=acc[:])
        b = [score(j, n_words, n_plane, j * BANK, (j + 1) * BANK, FP8X4, 4) for j in range(POOL // BANK)]

        s1 = sb.tile([P, SLOTS], F32, name="s1")
        for lo in (0, HALF):
            nc.scalar.activation(s1[:, lo : lo + HALF], a[:].indirect(offsets(l1, lo, lo + HALF)),
                                 ACT.Sigmoid, bias=thr_t[:], scale=slope_t[:])

        w_first = sb.tile([P, FIRST], F32, name="w_first")
        nc.vector.tensor_tensor(w_first[:], c0[:].indirect(offsets(l2, 0, FIRST)), s1[:, :FIRST], ALU.mult)
        c_rest = sb.tile([P, SLOTS - FIRST], F32, name="c_rest")
        nc.scalar.activation(c_rest[:], c0[:].indirect(offsets(l2, FIRST, SLOTS)), ACT.Copy)
        nc.vector.tensor_copy(f1[:].indirect(offsets(l3, 0, FIRST)), w_first[:])
        nc.vector.tensor_tensor(f1[:].indirect(offsets(l3, FIRST, SLOTS)), c_rest[:], s1[:, FIRST:], ALU.mult)

        late = sb.tile([P, SLOTS + SHARE], F32, name="late", tag="c0")
        a5 = late[:, :SLOTS]
        b_share = late[:, SLOTS:]
        nc.scalar.activation(a5, a[:].indirect(l5[:]), ACT.Copy)
        nc.scalar.copy(out=b_share, in_=b[1][:, BANK - SHARE :])

        cc = sb.tile([P, POOL], F32, name="cc")
        nc.gpsimd.tensor_tensor(cc[:, POOL - SHARE :], b_share, f1[:, POOL - SHARE :], ALU.add)
        nc.vector.tensor_tensor(cc[:, :BANK], b[0][:], f1[:, :BANK], ALU.add)
        nc.vector.tensor_tensor(cc[:, BANK : POOL - SHARE], b[1][:, : BANK - SHARE], f1[:, BANK : POOL - SHARE], ALU.add)

        c4 = sb.tile([P, SLOTS], F32, name="c4")
        nc.vector.tensor_copy(c4[:, :HALF], cc[:].indirect(offsets(l4, 0, HALF)))
        nc.scalar.activation(c4[:, HALF:], cc[:].indirect(offsets(l4, HALF, SLOTS)), ACT.Copy)
        y = sb.tile([P, SLOTS], F32, name="y")
        for lo, hi, queue in ((0, HALF, nc.sync), (HALF, SLOTS, nc.scalar)):
            nc.vector.tensor_tensor(y[:, lo:hi], c4[:, lo:hi], a5[:, lo:hi], ALU.max)
            queue.dma_start(out[:, lo:hi], y[:, lo:hi])
